import numpy as np
import ml_dtypes


def mxq(x, axis, fmt="e4m3"):
    dtype, down = {"e4m3": (ml_dtypes.float8_e4m3fn, 7), "e5m2": (ml_dtypes.float8_e5m2, 14)}[fmt]
    v = np.moveaxis(np.asarray(x, np.float32).astype(ml_dtypes.bfloat16).astype(np.float64), axis, -1)
    blocks = v.reshape(v.shape[:-1] + (-1, 32))
    amax = np.abs(blocks).max(-1, keepdims=True)
    byte = np.maximum(np.where(amax > 0, np.frexp(amax)[1] - 1 + 127, 0) - down, 1)
    scale = np.exp2(byte - 127.0)
    codes = (blocks / scale).astype(np.float32).astype(dtype).astype(np.float64)
    return np.moveaxis((codes * scale).reshape(v.shape), -1, axis)


WIDE = False


def mx_kscale(k):
    if not WIDE:
        return np.ones(k)
    levels = np.array([10, -10, 5, -5, 0])
    if k % 512:
        return np.exp2(np.random.permutation(np.resize(levels, k // 32))).repeat(32)
    a = np.empty((k // 512, 16))
    for p in range(k // 512):
        a[p, :8] = np.random.permutation(np.resize(levels, 8))
        for g in range(8):
            far = levels[np.abs(levels - a[p, g]) >= 10]
            a[p, g + 8] = far[np.random.randint(len(far))]
    return np.exp2(a.ravel()).repeat(32)


def f64(x):
    return np.asarray(x).astype(np.float64)


def striped(idx):
    return np.tile(idx.reshape(-1, 16).T, (8, 1)).astype(np.uint16)


def unstriped(offs):
    return offs[:16].T.reshape(-1).astype(np.int64)


def pack_weight(w):
    k, n = w.shape
    w = f64(np.asarray(w, np.float32).astype(ml_dtypes.bfloat16)).reshape(k // 32, 32, n)
    amax = np.abs(w).max(1)
    byte = np.clip(np.where(amax > 0, np.frexp(amax)[1] - 1 + 127 - 7, 1), 1, 254)
    scaled = (w * np.exp2(127.0 - byte)[:, None, :]).reshape(k, n).astype(np.float32)
    words = np.ascontiguousarray(scaled.reshape(k // 512, 128, 4, n).transpose(0, 1, 3, 2)).astype(ml_dtypes.float8_e4m3fn).view(np.uint8)
    return words, np.ascontiguousarray(byte.astype(np.uint8).reshape(k // 512, 16, n))


def unpack_weight(words, scales):
    g, p, n, _ = words.shape
    vals = np.ascontiguousarray(words).view(ml_dtypes.float8_e4m3fn).astype(np.float64) * np.repeat(np.exp2(scales.astype(np.float64) - 127.0), 8, axis=1)[..., None]
    return vals.transpose(0, 1, 3, 2).reshape(g * 512, n)


K, T, S, J = 1536, 1024, 512, 256


def setup_inputs():
    n = np.random.standard_normal
    s = mx_kscale(K)[:, None]
    packed_xT = pack_weight(n((K, T)) * s)
    return {
        "x_words": packed_xT[0],
        "x_scales": packed_xT[1],
        "hT": (n((K, J)) / np.sqrt(K) / s).astype(np.float32),
        "offs": striped(np.random.permutation(T)[:S]),
    }


def reference(x_words, x_scales, hT, offs):
    hTq = mxq(f64(hT), 0, "e4m3")
    xq = unpack_weight(x_words, x_scales)[:, unstriped(offs)]
    y = hTq.T @ xq
    e = np.exp(y - y.max(axis=1, keepdims=True))
    p = e / e.sum(axis=1, keepdims=True)
    out = np.zeros((J, T))
    out[:, unstriped(offs)] = p
    return out

@@ -1,0 +1,140 @@
+from contextlib import ExitStack
+
+import concourse.mybir as mybir
+
+K, T, S, J = 1536, 1024, 512, 256
+FLOPS = 2 * K * S * J
+
+F32 = mybir.dt.float32
+BF16 = mybir.dt.bfloat16
+I32 = mybir.dt.int32
+U32 = mybir.dt.uint32
+U16 = mybir.dt.uint16
+U8 = mybir.dt.uint8
+FP8X4 = mybir.dt.float8_e4m3fn_x4
+ACT = mybir.ActivationFunctionType
+ALU = mybir.AluOpType
+AX = mybir.AxisListType
+
+P = 128
+PACK = 4
+PASSES = K // (P * PACK)
+HALF = S // 2
+
+
+def interleave(copy, grouped, raw):
+    copy(
+        out=grouped.rearrange("p (c i) t -> p c t i", i=4),
+        in_=raw.rearrange("p t (c i) -> p c t i", i=4),
+    )
+
+
+def tile_picked_zvoc_soft_p_kernel(tc, x_words, x_scales, hT, offs, out):
+    nc = tc.nc
+    with ExitStack() as ctx:
+        keep = ctx.enter_context(tc.tile_pool(name="keep", bufs=1))
+        psum = ctx.enter_context(tc.psum_pool(name="psum", bufs=1))
+
+        offsets = keep.tile([P, S // 16], U16, name="offsets")
+        nc.sync.dma_start(offsets[:], offs)
+
+        scale_table = keep.tile([P, T], U8, name="scale_table", align_bytes=64)
+        nc.gpsimd.memset(scale_table[:].bitcast(I32), 0)
+        for q in range(4):
+            nc.gpsimd.dma_start(
+                out=scale_table[32 * q : 32 * q + 4 * PASSES, :].bitcast(I32),
+                in_=x_scales[:, 4 * q : 4 * q + 4, :].bitcast(I32),
+            )
+
+        word_tables, h_raw = [], []
+        for g in range(PASSES):
+            table = keep.tile([P, T], I32, name=f"word_table{g}", align_bytes=64)
+            nc.sync.dma_start(out=table[:], in_=x_words[g].rearrange("p n t -> p (n t)").bitcast(I32))
+            word_tables.append(table)
+            raw = keep.tile([P, PACK, J], F32, name=f"h_raw{g}", align_bytes=64)
+            nc.sync.dma_start(
+                out=raw[:], in_=hT[g * P * PACK : (g + 1) * P * PACK, :].rearrange("(p t) m -> p t m", t=PACK)
+            )
+            h_raw.append(raw)
+
+        windows = []
+        for m in range(2):
+            window = keep.tile([P, T], F32, name=f"window{m}", align_bytes=64)
+            nc.vector.memset(window[:], 0.0)
+            windows.append(window)
+
+        warm = keep.tile([P, 1], F32, name="warm")
+        nc.scalar.activation(out=warm[:], in_=windows[0][:, 0:1], func=ACT.Exp)
+
+        x_codes = [keep.tile([P, S], U32, name=f"x_codes{g}", align_bytes=64) for g in range(PASSES)]
+        x_planes = keep.tile([P, S], U8, name="x_planes", align_bytes=64)
+        h_codes = [keep.tile([P, J], U32, name=f"h_codes{g}", align_bytes=64) for g in range(PASSES)]
+        h_planes = [keep.tile([P, J], U8, name=f"h_planes{g}", align_bytes=64) for g in range(PASSES)]
+        logits = [psum.tile([P, S], F32, name=f"logits{m}") for m in range(2)]
+
+        def gather_words(g):
+            nc.vector.tensor_copy(x_codes[g][:], word_tables[g][:].bitcast(U32).indirect(offsets[:]))
+
+        def quantise(g, cols, copy, name):
+            width = cols.stop - cols.start
+            grouped = keep.tile([P, width, PACK], BF16, name=name, align_bytes=64)
+            interleave(copy, grouped[:], h_raw[g][:, :, cols])
+            nc.vector.quantize_mx(
+                out=h_codes[g][:, cols].bitcast(FP8X4),
+                scales=h_planes[g][:, cols],
+                in_=grouped[:].rearrange("p c t -> p (c t)"),
+            )
+
+        def multiply(g, m):
+            cols = slice(m * P, (m + 1) * P)
+            nc.tensor.matmul_mx(
+                out=logits[m][:],
+                lhsT=h_codes[g][:, cols].bitcast(FP8X4),
+                lhsT_scale=h_planes[g][:, cols],
+                rhs=x_codes[g][:].bitcast(FP8X4),
+                rhs_scale=x_planes[4 * g :, :],
+                start=(g == 0),
+                stop=(g == PASSES - 1),
+            )
+
+        gather_words(0)
+        quantise(0, slice(0, J), nc.scalar.copy, "grouped0")
+        gather_words(1)
+        nc.vector.tensor_copy(x_planes[:], scale_table[:].indirect(offsets[:]))
+        quantise(1, slice(0, J), nc.scalar.copy, "grouped1")
+        gather_words(2)
+        quantise(2, slice(0, P), nc.vector.tensor_copy, "grouped2a")
+        quantise(2, slice(P, J), nc.scalar.copy, "grouped2b")
+        for g in range(PASSES):
+            for m in range(2):
+                multiply(g, m)
+
+        neg_max0 = keep.tile([P, 1], F32, name="neg_max0")
+        shared = keep.tile([P, 1], F32, name="shared")
+        nc.vector.tensor_reduce(out=neg_max0[:], in_=logits[0][:], axis=AX.X, op=ALU.max, negate=True)
+        nc.vector.tensor_reduce(out=shared[:], in_=logits[1][:], axis=AX.X, op=ALU.max, negate=True)
+
+        e0a = keep.tile([P, HALF], F32, name="e0a")
+        e0b = keep.tile([P, HALF], F32, name="e0b")
+        e1 = keep.tile([P, S], F32, name="e1")
+        sum0a = keep.tile([P, 1], F32, name="sum0a")
+        sum0 = keep.tile([P, 1], F32, name="sum0")
+        sum1 = keep.tile([P, 1], F32, name="sum1")
+        inv0 = keep.tile([P, 1], F32, name="inv0")
+        inv1 = keep.tile([P, 1], F32, name="inv1")
+        p1 = keep.tile([P, S], F32, name="p1")
+        rows0 = keep.tile([P, T], F32, name="rows0")
+
+        nc.scalar.activation(out=e0a[:], in_=logits[0][:, :HALF], func=ACT.Exp, bias=neg_max0[:], accum_out=sum0a[:])
+        nc.vector.tensor_copy(windows[0][:].indirect(offsets[:, : HALF // 16]), e0a[:])
+        nc.scalar.activation(out=e1[:], in_=logits[1][:], func=ACT.Exp, bias=shared[:], accum_out=sum1[:])
+        nc.vector.reciprocal(out=inv1[:], in_=sum1[:])
+        nc.scalar.activation(out=e0b[:], in_=logits[0][:, HALF:], func=ACT.Exp, bias=neg_max0[:], accum_out=shared[:])
+        nc.scalar.activation(out=sum0[:], in_=sum0a[:], func=ACT.Identity, bias=shared[:])
+        nc.vector.tensor_copy(windows[0][:].indirect(offsets[:, HALF // 16 :]), e0b[:])
+        nc.scalar.activation(out=p1[:], in_=e1[:], func=ACT.Copy, scale=inv1[:])
+        nc.vector.reciprocal(out=inv0[:], in_=sum0[:])
+        nc.vector.tensor_copy(windows[1][:].indirect(offsets[:]), p1[:])
+        nc.scalar.activation(out=rows0[:], in_=windows[0][:], func=ACT.Copy, scale=inv0[:])
+        nc.sync.dma_start(out=out[0:P, :], in_=rows0[:])
+        nc.sync.dma_start(out=out[P:J, :], in_=windows[1][:])

@@ -38,24 +38,34 @@ def tile_picked_zvoc_soft_p_kernel(tc, x_words, x_scales, hT, offs, out):
         offsets = keep.tile([P, S // 16], U16, name="offsets")
         nc.sync.dma_start(offsets[:], offs)
 
+        word_tables, h_raw = {}, {}
+
+        def load_words(g, slot):
+            table = keep.tile([P, T], I32, name=f"word_table{g}", tag=slot, align_bytes=64)
+            nc.sync.dma_start(out=table[:], in_=x_words[g].rearrange("p n t -> p (n t)").bitcast(I32))
+            word_tables[g] = table
+
+        def load_hidden(g, slot):
+            raw = keep.tile([P, PACK, J], F32, name=f"h_raw{g}", tag=slot, align_bytes=64)
+            nc.sync.dma_start(
+                out=raw[:], in_=hT[g * P * PACK : (g + 1) * P * PACK, :].rearrange("(p t) m -> p t m", t=PACK)
+            )
+            h_raw[g] = raw
+
+        load_words(0, "slot0")
+        load_words(1, "slot1")
+        load_hidden(0, "slot2")
         scale_table = keep.tile([P, T], U8, name="scale_table", align_bytes=64)
         nc.gpsimd.memset(scale_table[:].bitcast(I32), 0)
         for q in range(4):
-            nc.gpsimd.dma_start(
+            (nc.scalar if q < 2 else nc.sync).dma_start(
                 out=scale_table[32 * q : 32 * q + 4 * PASSES, :].bitcast(I32),
                 in_=x_scales[:, 4 * q : 4 * q + 4, :].bitcast(I32),
             )
 
-        word_tables, h_raw = [], []
-        for g in range(PASSES):
-            table = keep.tile([P, T], I32, name=f"word_table{g}", align_bytes=64)
-            nc.sync.dma_start(out=table[:], in_=x_words[g].rearrange("p n t -> p (n t)").bitcast(I32))
-            word_tables.append(table)
-            raw = keep.tile([P, PACK, J], F32, name=f"h_raw{g}", align_bytes=64)
-            nc.sync.dma_start(
-                out=raw[:], in_=hT[g * P * PACK : (g + 1) * P * PACK, :].rearrange("(p t) m -> p t m", t=PACK)
-            )
-            h_raw.append(raw)
+        load_hidden(1, "slot3")
+        load_words(2, "slot4")
+        load_hidden(2, "slot5")
 
         windows = []
         for m in range(2):
@@ -98,10 +108,11 @@ def tile_picked_zvoc_soft_p_kernel(tc, x_words, x_scales, hT, offs, out):
             )
 
         gather_words(0)
-        quantise(0, slice(0, J), nc.scalar.copy, "grouped0")
         gather_words(1)
         nc.vector.tensor_copy(x_planes[:], scale_table[:].indirect(offsets[:]))
-        quantise(1, slice(0, J), nc.scalar.copy, "grouped1")
+        quantise(0, slice(0, J), nc.scalar.copy, "grouped0")
+        quantise(1, slice(0, P), nc.vector.tensor_copy, "grouped1a")
+        quantise(1, slice(P, J), nc.scalar.copy, "grouped1b")
         gather_words(2)
         quantise(2, slice(0, P), nc.vector.tensor_copy, "grouped2a")
         quantise(2, slice(P, J), nc.scalar.copy, "grouped2b")
@@ -130,7 +141,7 @@ def tile_picked_zvoc_soft_p_kernel(tc, x_words, x_scales, hT, offs, out):
         nc.scalar.activation(out=e1[:], in_=logits[1][:], func=ACT.Exp, bias=shared[:], accum_out=sum1[:])
         nc.vector.reciprocal(out=inv1[:], in_=sum1[:])
         nc.scalar.activation(out=e0b[:], in_=logits[0][:, HALF:], func=ACT.Exp, bias=neg_max0[:], accum_out=shared[:])
-        nc.scalar.activation(out=sum0[:], in_=sum0a[:], func=ACT.Identity, bias=shared[:])
+        nc.vector.tensor_tensor(out=sum0[:], in0=sum0a[:], in1=shared[:], op=ALU.add)
         nc.vector.tensor_copy(windows[0][:].indirect(offsets[:, HALF // 16 :]), e0b[:])
         nc.scalar.activation(out=p1[:], in_=e1[:], func=ACT.Copy, scale=inv1[:])
         nc.vector.reciprocal(out=inv0[:], in_=sum0[:])

@@ -147,5 +147,5 @@ def tile_picked_zvoc_soft_p_kernel(tc, x_words, x_scales, hT, offs, out):
         nc.vector.reciprocal(out=inv0[:], in_=sum0[:])
         nc.vector.tensor_copy(windows[1][:].indirect(offsets[:]), p1[:])
         nc.scalar.activation(out=rows0[:], in_=windows[0][:], func=ACT.Copy, scale=inv0[:])
-        nc.sync.dma_start(out=out[0:P, :], in_=rows0[:])
+        nc.scalar.dma_start(out=out[0:P, :], in_=rows0[:])
         nc.sync.dma_start(out=out[P:J, :], in_=windows[1][:])

@@ -52,17 +52,17 @@ def tile_picked_zvoc_soft_p_kernel(tc, x_words, x_scales, hT, offs, out):
             )
             h_raw[g] = raw
 
-        load_words(0, "slot0")
-        load_words(1, "slot1")
-        load_hidden(0, "slot2")
         scale_table = keep.tile([P, T], U8, name="scale_table", align_bytes=64)
-        nc.gpsimd.memset(scale_table[:].bitcast(I32), 0)
+        nc.vector.memset(scale_table[:].bitcast(I32), 0)
+        load_words(0, "slot0")
+        load_hidden(0, "slot2")
         for q in range(4):
             (nc.scalar if q < 2 else nc.sync).dma_start(
                 out=scale_table[32 * q : 32 * q + 4 * PASSES, :].bitcast(I32),
                 in_=x_scales[:, 4 * q : 4 * q + 4, :].bitcast(I32),
             )
 
+        load_words(1, "slot1")
         load_hidden(1, "slot3")
         load_words(2, "slot4")
         load_hidden(2, "slot5")
@@ -108,10 +108,10 @@ def tile_picked_zvoc_soft_p_kernel(tc, x_words, x_scales, hT, offs, out):
             )
 
         gather_words(0)
-        gather_words(1)
         nc.vector.tensor_copy(x_planes[:], scale_table[:].indirect(offsets[:]))
         quantise(0, slice(0, J), nc.scalar.copy, "grouped0")
-        quantise(1, slice(0, P), nc.vector.tensor_copy, "grouped1a")
+        gather_words(1)
+        quantise(1, slice(0, P), nc.scalar.copy, "grouped1a")
         quantise(1, slice(P, J), nc.scalar.copy, "grouped1b")
         gather_words(2)
         quantise(2, slice(0, P), nc.vector.tensor_copy, "grouped2a")

@@ -73,9 +73,6 @@ def tile_picked_zvoc_soft_p_kernel(tc, x_words, x_scales, hT, offs, out):
             nc.vector.memset(window[:], 0.0)
             windows.append(window)
 
-        warm = keep.tile([P, 1], F32, name="warm")
-        nc.scalar.activation(out=warm[:], in_=windows[0][:, 0:1], func=ACT.Exp)
-
         x_codes = [keep.tile([P, S], U32, name=f"x_codes{g}", align_bytes=64) for g in range(PASSES)]
         x_planes = keep.tile([P, S], U8, name="x_planes", align_bytes=64)
         h_codes = [keep.tile([P, J], U32, name=f"h_codes{g}", align_bytes=64) for g in range(PASSES)]

@@ -20,6 +20,8 @@ P = 128
 PACK = 4
 PASSES = K // (P * PACK)
 HALF = S // 2
+UNPICKED = -(2.0**127)
+CHUNKS = (slice(0, 128), slice(128, 256), slice(256, 512))
 
 
 def interleave(copy, grouped, raw):
@@ -62,25 +64,30 @@ def tile_picked_zvoc_soft_p_kernel(tc, x_words, x_scales, hT, offs, out):
                 in_=x_scales[:, 4 * q : 4 * q + 4, :].bitcast(I32),
             )
 
-        load_words(1, "slot1")
         load_hidden(1, "slot3")
-        load_words(2, "slot4")
+        load_words(1, "slot1")
         load_hidden(2, "slot5")
+        load_words(2, "slot4")
 
-        windows = []
-        for m in range(2):
-            window = keep.tile([P, T], F32, name=f"window{m}", align_bytes=64)
-            nc.vector.memset(window[:], 0.0)
-            windows.append(window)
+        window0 = keep.tile([P, T], F32, name="window0", align_bytes=64)
+        nc.vector.memset(window0[:], UNPICKED)
+        window1 = keep.tile([P, T], F32, name="window1", align_bytes=64)
+        nc.vector.memset(window1[:], 0.0)
+        minus_one = keep.tile([P, 1], F32, name="minus_one")
+        nc.gpsimd.memset(minus_one[:], -1.0)
 
         x_codes = [keep.tile([P, S], U32, name=f"x_codes{g}", align_bytes=64) for g in range(PASSES)]
         x_planes = keep.tile([P, S], U8, name="x_planes", align_bytes=64)
         h_codes = [keep.tile([P, J], U32, name=f"h_codes{g}", align_bytes=64) for g in range(PASSES)]
         h_planes = [keep.tile([P, J], U8, name=f"h_planes{g}", align_bytes=64) for g in range(PASSES)]
-        logits = [psum.tile([P, S], F32, name=f"logits{m}") for m in range(2)]
+        logits0 = [psum.tile([P, c.stop - c.start], F32, name=f"logits0_{i}") for i, c in enumerate(CHUNKS)]
+        logits1 = psum.tile([P, S], F32, name="logits1")
 
-        def gather_words(g):
-            nc.vector.tensor_copy(x_codes[g][:], word_tables[g][:].bitcast(U32).indirect(offsets[:]))
+        def listed(entries):
+            return offsets[:, entries.start // 16 : entries.stop // 16]
+
+        def gather_words(g, entries):
+            nc.vector.tensor_copy(x_codes[g][:, entries], word_tables[g][:].bitcast(U32).indirect(listed(entries)))
 
         def quantise(g, cols, copy, name):
             width = cols.stop - cols.start
@@ -92,40 +99,41 @@ def tile_picked_zvoc_soft_p_kernel(tc, x_words, x_scales, hT, offs, out):
                 in_=grouped[:].rearrange("p c t -> p (c t)"),
             )
 
-        def multiply(g, m):
+        def multiply(g, m, bank, entries):
             cols = slice(m * P, (m + 1) * P)
             nc.tensor.matmul_mx(
-                out=logits[m][:],
+                out=bank[:],
                 lhsT=h_codes[g][:, cols].bitcast(FP8X4),
                 lhsT_scale=h_planes[g][:, cols],
-                rhs=x_codes[g][:].bitcast(FP8X4),
-                rhs_scale=x_planes[4 * g :, :],
+                rhs=x_codes[g][:, entries].bitcast(FP8X4),
+                rhs_scale=x_planes[4 * g :, entries],
                 start=(g == 0),
                 stop=(g == PASSES - 1),
             )
 
-        gather_words(0)
+        whole = slice(0, S)
+        gather_words(0, whole)
         nc.vector.tensor_copy(x_planes[:], scale_table[:].indirect(offsets[:]))
         quantise(0, slice(0, J), nc.scalar.copy, "grouped0")
-        gather_words(1)
-        quantise(1, slice(0, P), nc.scalar.copy, "grouped1a")
-        quantise(1, slice(P, J), nc.scalar.copy, "grouped1b")
-        gather_words(2)
+        quantise(1, slice(0, J), nc.scalar.copy, "grouped1")
+        gather_words(1, whole)
         quantise(2, slice(0, P), nc.vector.tensor_copy, "grouped2a")
         quantise(2, slice(P, J), nc.scalar.copy, "grouped2b")
-        for g in range(PASSES):
-            for m in range(2):
-                multiply(g, m)
+        for entries in CHUNKS:
+            gather_words(2, entries)
+        for g in range(PASSES - 1):
+            for bank, entries in zip(logits0, CHUNKS):
+                multiply(g, 0, bank, entries)
+            multiply(g, 1, logits1, whole)
+        multiply(2, 0, logits0[0], CHUNKS[0])
+        multiply(2, 0, logits0[1], CHUNKS[1])
+        multiply(2, 1, logits1, whole)
+        multiply(2, 0, logits0[2], CHUNKS[2])
 
+        y0 = keep.tile([P, S], F32, name="y0")
         neg_max0 = keep.tile([P, 1], F32, name="neg_max0")
-        shared = keep.tile([P, 1], F32, name="shared")
-        nc.vector.tensor_reduce(out=neg_max0[:], in_=logits[0][:], axis=AX.X, op=ALU.max, negate=True)
-        nc.vector.tensor_reduce(out=shared[:], in_=logits[1][:], axis=AX.X, op=ALU.max, negate=True)
-
-        e0a = keep.tile([P, HALF], F32, name="e0a")
-        e0b = keep.tile([P, HALF], F32, name="e0b")
-        e1 = keep.tile([P, S], F32, name="e1")
-        sum0a = keep.tile([P, 1], F32, name="sum0a")
+        neg_max1 = keep.tile([P, 1], F32, name="neg_max1")
+        e1 = keep.tile([P, S], F32, name="e1", tag="exps")
         sum0 = keep.tile([P, 1], F32, name="sum0")
         sum1 = keep.tile([P, 1], F32, name="sum1")
         inv0 = keep.tile([P, 1], F32, name="inv0")
@@ -133,16 +141,25 @@ def tile_picked_zvoc_soft_p_kernel(tc, x_words, x_scales, hT, offs, out):
         p1 = keep.tile([P, S], F32, name="p1")
         rows0 = keep.tile([P, T], F32, name="rows0")
 
-        nc.scalar.activation(out=e0a[:], in_=logits[0][:, :HALF], func=ACT.Exp, bias=neg_max0[:], accum_out=sum0a[:])
-        nc.vector.tensor_copy(windows[0][:].indirect(offsets[:, : HALF // 16]), e0a[:])
-        nc.scalar.activation(out=e1[:], in_=logits[1][:], func=ACT.Exp, bias=shared[:], accum_out=sum1[:])
-        nc.vector.reciprocal(out=inv1[:], in_=sum1[:])
-        nc.scalar.activation(out=e0b[:], in_=logits[0][:, HALF:], func=ACT.Exp, bias=neg_max0[:], accum_out=shared[:])
-        nc.vector.tensor_tensor(out=sum0[:], in0=sum0a[:], in1=shared[:], op=ALU.add)
-        nc.vector.tensor_copy(windows[0][:].indirect(offsets[:, HALF // 16 :]), e0b[:])
+        for bank, entries in zip(logits0, CHUNKS):
+            nc.scalar.copy(out=y0[:, entries], in_=bank[:])
+        for entries in CHUNKS[:2]:
+            nc.vector.tensor_copy(window0[:].indirect(listed(entries)), y0[:, entries])
+        nc.vector.tensor_reduce(out=neg_max1[:], in_=logits1[:], axis=AX.X, op=ALU.max, negate=True)
+        nc.vector.tensor_reduce(out=neg_max0[:], in_=y0[:], axis=AX.X, op=ALU.max, negate=True)
+        nc.vector.tensor_copy(window0[:].indirect(listed(CHUNKS[2])), y0[:, CHUNKS[2]])
+
+        nc.scalar.activation(out=e1[:], in_=logits1[:], func=ACT.Exp, bias=neg_max1[:], accum_out=sum1[:])
+        nc.gpsimd.tensor_tensor(out=inv1[:], in0=sum1[:], in1=minus_one[:], op=ALU.pow)
+        listed0 = keep.tile([P, S], F32, name="listed0")
+        nc.scalar.activation(out=listed0[:], in_=y0[:], func=ACT.Exp, bias=neg_max0[:], accum_out=sum0[:])
+        nc.gpsimd.tensor_tensor(out=inv0[:], in0=sum0[:], in1=minus_one[:], op=ALU.pow)
         nc.scalar.activation(out=p1[:], in_=e1[:], func=ACT.Copy, scale=inv1[:])
-        nc.vector.reciprocal(out=inv0[:], in_=sum0[:])
-        nc.vector.tensor_copy(windows[1][:].indirect(offsets[:]), p1[:])
-        nc.scalar.activation(out=rows0[:], in_=windows[0][:], func=ACT.Copy, scale=inv0[:])
-        nc.scalar.dma_start(out=out[0:P, :], in_=rows0[:])
-        nc.sync.dma_start(out=out[P:J, :], in_=windows[1][:])
+        nc.vector.tensor_copy(window1[:].indirect(offsets[:]), p1[:])
+
+        e0 = keep.tile([P, T], F32, name="e0", tag="exps")
+        for cols in (slice(0, T // 2), slice(T // 2, T)):
+            nc.scalar.activation(out=e0[:, cols], in_=window0[:, cols], func=ACT.Exp, bias=neg_max0[:])
+            nc.scalar.activation(out=rows0[:, cols], in_=e0[:, cols], func=ACT.Copy, scale=inv0[:])
+            nc.scalar.dma_start(out=out[0:P, cols], in_=rows0[:, cols])
+        nc.sync.dma_start(out=out[P:J, :], in_=window1[:])

@@ -38,7 +38,6 @@ def tile_picked_zvoc_soft_p_kernel(tc, x_words, x_scales, hT, offs, out):
         psum = ctx.enter_context(tc.psum_pool(name="psum", bufs=1))
 
         offsets = keep.tile([P, S // 16], U16, name="offsets")
-        nc.sync.dma_start(offsets[:], offs)
 
         word_tables, h_raw = {}, {}
 
@@ -57,6 +56,7 @@ def tile_picked_zvoc_soft_p_kernel(tc, x_words, x_scales, hT, offs, out):
         scale_table = keep.tile([P, T], U8, name="scale_table", align_bytes=64)
         nc.vector.memset(scale_table[:].bitcast(I32), 0)
         load_words(0, "slot0")
+        nc.sync.dma_start(offsets[:], offs)
         load_hidden(0, "slot2")
         for q in range(4):
             (nc.scalar if q < 2 else nc.sync).dma_start(
@@ -89,10 +89,13 @@ def tile_picked_zvoc_soft_p_kernel(tc, x_words, x_scales, hT, offs, out):
         def gather_words(g, entries):
             nc.vector.tensor_copy(x_codes[g][:, entries], word_tables[g][:].bitcast(U32).indirect(listed(entries)))
 
-        def quantise(g, cols, copy, name):
+        def regroup(g, cols, copy):
             width = cols.stop - cols.start
-            grouped = keep.tile([P, width, PACK], BF16, name=name, align_bytes=64)
+            grouped = keep.tile([P, width, PACK], BF16, name=f"grouped{g}_{cols.start}", align_bytes=64)
             interleave(copy, grouped[:], h_raw[g][:, :, cols])
+            return grouped
+
+        def quantise(g, cols, grouped):
             nc.vector.quantize_mx(
                 out=h_codes[g][:, cols].bitcast(FP8X4),
                 scales=h_planes[g][:, cols],
@@ -114,20 +117,23 @@ def tile_picked_zvoc_soft_p_kernel(tc, x_words, x_scales, hT, offs, out):
         whole = slice(0, S)
         gather_words(0, whole)
         nc.vector.tensor_copy(x_planes[:], scale_table[:].indirect(offsets[:]))
-        quantise(0, slice(0, J), nc.scalar.copy, "grouped0")
-        quantise(1, slice(0, J), nc.scalar.copy, "grouped1")
+        both, tile0, tile1 = slice(0, J), slice(0, P), slice(P, J)
+        quantise(0, both, regroup(0, both, nc.scalar.copy))
+        quantise(1, tile0, regroup(1, tile0, nc.scalar.copy))
         gather_words(1, whole)
-        quantise(2, slice(0, P), nc.vector.tensor_copy, "grouped2a")
-        quantise(2, slice(P, J), nc.scalar.copy, "grouped2b")
-        for entries in CHUNKS:
-            gather_words(2, entries)
+        last0 = regroup(2, tile0, nc.vector.tensor_copy)
+        quantise(1, tile1, regroup(1, tile1, nc.scalar.copy))
+        quantise(2, tile0, last0)
+        quantise(2, tile1, regroup(2, tile1, nc.scalar.copy))
+        gather_words(2, CHUNKS[0])
+        gather_words(2, slice(CHUNKS[0].stop, S))
         for g in range(PASSES - 1):
             for bank, entries in zip(logits0, CHUNKS):
                 multiply(g, 0, bank, entries)
             multiply(g, 1, logits1, whole)
         multiply(2, 0, logits0[0], CHUNKS[0])
-        multiply(2, 0, logits0[1], CHUNKS[1])
         multiply(2, 1, logits1, whole)
+        multiply(2, 0, logits0[1], CHUNKS[1])
         multiply(2, 0, logits0[2], CHUNKS[2])
 
         y0 = keep.tile([P, S], F32, name="y0")
@@ -143,9 +149,9 @@ def tile_picked_zvoc_soft_p_kernel(tc, x_words, x_scales, hT, offs, out):
 
         for bank, entries in zip(logits0, CHUNKS):
             nc.scalar.copy(out=y0[:, entries], in_=bank[:])
-        for entries in CHUNKS[:2]:
-            nc.vector.tensor_copy(window0[:].indirect(listed(entries)), y0[:, entries])
+        nc.vector.tensor_copy(window0[:].indirect(listed(CHUNKS[0])), y0[:, CHUNKS[0]])
         nc.vector.tensor_reduce(out=neg_max1[:], in_=logits1[:], axis=AX.X, op=ALU.max, negate=True)
+        nc.vector.tensor_copy(window0[:].indirect(listed(CHUNKS[1])), y0[:, CHUNKS[1]])
         nc.vector.tensor_reduce(out=neg_max0[:], in_=y0[:], axis=AX.X, op=ALU.max, negate=True)
         nc.vector.tensor_copy(window0[:].indirect(listed(CHUNKS[2])), y0[:, CHUNKS[2]])
 
@@ -161,5 +167,5 @@ def tile_picked_zvoc_soft_p_kernel(tc, x_words, x_scales, hT, offs, out):
         for cols in (slice(0, T // 2), slice(T // 2, T)):
             nc.scalar.activation(out=e0[:, cols], in_=window0[:, cols], func=ACT.Exp, bias=neg_max0[:])
             nc.scalar.activation(out=rows0[:, cols], in_=e0[:, cols], func=ACT.Copy, scale=inv0[:])
-            nc.scalar.dma_start(out=out[0:P, cols], in_=rows0[:, cols])
-        nc.sync.dma_start(out=out[P:J, :], in_=window1[:])
+            nc.sync.dma_start(out=out[0:P, cols], in_=rows0[:, cols])
+        nc.scalar.dma_start(out=out[P:J, :], in_=window1[:])

@@ -21,6 +21,7 @@ PACK = 4
 PASSES = K // (P * PACK)
 HALF = S // 2
 UNPICKED = -(2.0**127)
+PIECES = (slice(0, 384), slice(384, 768), slice(768, 1024))
 CHUNKS = (slice(0, 128), slice(128, 256), slice(256, 512))
 
 
@@ -164,8 +165,12 @@ def tile_picked_zvoc_soft_p_kernel(tc, x_words, x_scales, hT, offs, out):
         nc.vector.tensor_copy(window1[:].indirect(offsets[:]), p1[:])
 
         e0 = keep.tile([P, T], F32, name="e0", tag="exps")
-        for cols in (slice(0, T // 2), slice(T // 2, T)):
-            nc.scalar.activation(out=e0[:, cols], in_=window0[:, cols], func=ACT.Exp, bias=neg_max0[:])
-            nc.scalar.activation(out=rows0[:, cols], in_=e0[:, cols], func=ACT.Copy, scale=inv0[:])
-            nc.sync.dma_start(out=out[0:P, cols], in_=rows0[:, cols])
+        for i in range(len(PIECES) + 1):
+            if i < len(PIECES):
+                cols = PIECES[i]
+                nc.scalar.activation(out=e0[:, cols], in_=window0[:, cols], func=ACT.Exp, bias=neg_max0[:])
+            if i > 0:
+                cols = PIECES[i - 1]
+                nc.scalar.activation(out=rows0[:, cols], in_=e0[:, cols], func=ACT.Copy, scale=inv0[:])
+                nc.sync.dma_start(out=out[0:P, cols], in_=rows0[:, cols])
         nc.scalar.dma_start(out=out[P:J, :], in_=window1[:])

@@ -43,18 +43,18 @@ def tile_picked_zvoc_soft_p_kernel(tc, x_words, x_scales, hT, offs, out):
         word_tables, h_raw = {}, {}
 
         def load_words(g, slot):
-            table = keep.tile([P, T], I32, name=f"word_table{g}", tag=slot, align_bytes=64)
+            table = keep.tile([P, T], I32, name=f"word_table{g}", tag=slot, align_bytes=256)
             nc.sync.dma_start(out=table[:], in_=x_words[g].rearrange("p n t -> p (n t)").bitcast(I32))
             word_tables[g] = table
 
         def load_hidden(g, slot):
-            raw = keep.tile([P, PACK, J], F32, name=f"h_raw{g}", tag=slot, align_bytes=64)
+            raw = keep.tile([P, PACK, J], F32, name=f"h_raw{g}", tag=slot, align_bytes=256)
             nc.sync.dma_start(
                 out=raw[:], in_=hT[g * P * PACK : (g + 1) * P * PACK, :].rearrange("(p t) m -> p t m", t=PACK)
             )
             h_raw[g] = raw
 
-        scale_table = keep.tile([P, T], U8, name="scale_table", align_bytes=64)
+        scale_table = keep.tile([P, T], U8, name="scale_table", align_bytes=256)
         nc.vector.memset(scale_table[:].bitcast(I32), 0)
         load_words(0, "slot0")
         nc.sync.dma_start(offsets[:], offs)
@@ -70,9 +70,9 @@ def tile_picked_zvoc_soft_p_kernel(tc, x_words, x_scales, hT, offs, out):
         load_hidden(2, "slot5")
         load_words(2, "slot4")
 
-        window0 = keep.tile([P, T], F32, name="window0", align_bytes=64)
+        window0 = keep.tile([P, T], F32, name="window0", align_bytes=256)
         nc.vector.memset(window0[:], UNPICKED)
-        window1 = keep.tile([P, T], F32, name="window1", align_bytes=64)
+        window1 = keep.tile([P, T], F32, name="window1", align_bytes=256)
         nc.vector.memset(window1[:], 0.0)
         minus_one = keep.tile([P, 1], F32, name="minus_one")
         nc.gpsimd.memset(minus_one[:], -1.0)
@@ -146,7 +146,7 @@ def tile_picked_zvoc_soft_p_kernel(tc, x_words, x_scales, hT, offs, out):
         inv0 = keep.tile([P, 1], F32, name="inv0")
         inv1 = keep.tile([P, 1], F32, name="inv1")
         p1 = keep.tile([P, S], F32, name="p1")
-        rows0 = keep.tile([P, T], F32, name="rows0")
+        rows0 = keep.tile([P, T], F32, name="rows0", align_bytes=256)
 
         for bank, entries in zip(logits0, CHUNKS):
             nc.scalar.copy(out=y0[:, entries], in_=bank[:])

@@ -21,7 +21,7 @@ PACK = 4
 PASSES = K // (P * PACK)
 HALF = S // 2
 UNPICKED = -(2.0**127)
-PIECES = (slice(0, 384), slice(384, 768), slice(768, 1024))
+PIECES = (slice(0, 512), slice(512, 1024))
 CHUNKS = (slice(0, 128), slice(128, 256), slice(256, 512))
 
 
@@ -172,5 +172,6 @@ def tile_picked_zvoc_soft_p_kernel(tc, x_words, x_scales, hT, offs, out):
             if i > 0:
                 cols = PIECES[i - 1]
                 nc.scalar.activation(out=rows0[:, cols], in_=e0[:, cols], func=ACT.Copy, scale=inv0[:])
-                nc.sync.dma_start(out=out[0:P, cols], in_=rows0[:, cols])
-        nc.scalar.dma_start(out=out[P:J, :], in_=window1[:])
+                nc.scalar.dma_start(out=out[0:P, cols], in_=rows0[:, cols])
+        nc.sync.dma_start(out=out[P:J:2, :], in_=window1[0:P:2, :])
+        nc.scalar.dma_start(out=out[P + 1 : J : 2, :], in_=window1[1:P:2, :])

@@ -19,17 +19,8 @@ AX = mybir.AxisListType
 P = 128
 PACK = 4
 PASSES = K // (P * PACK)
-HALF = S // 2
-UNPICKED = -(2.0**127)
-PIECES = (slice(0, 512), slice(512, 1024))
-CHUNKS = (slice(0, 128), slice(128, 256), slice(256, 512))
-
-
-def interleave(copy, grouped, raw):
-    copy(
-        out=grouped.rearrange("p (c i) t -> p c t i", i=4),
-        in_=raw.rearrange("p t (c i) -> p c t i", i=4),
-    )
+HALVES = (slice(0, S // 2), slice(S // 2, S))
+COLUMN_HALVES = (slice(0, T // 2), slice(T // 2, T))
 
 
 def tile_picked_zvoc_soft_p_kernel(tc, x_words, x_scales, hT, offs, out):
@@ -39,41 +30,34 @@ def tile_picked_zvoc_soft_p_kernel(tc, x_words, x_scales, hT, offs, out):
         psum = ctx.enter_context(tc.psum_pool(name="psum", bufs=1))
 
         offsets = keep.tile([P, S // 16], U16, name="offsets")
-
-        word_tables, h_raw = {}, {}
-
-        def load_words(g, slot):
-            table = keep.tile([P, T], I32, name=f"word_table{g}", tag=slot, align_bytes=256)
-            nc.sync.dma_start(out=table[:], in_=x_words[g].rearrange("p n t -> p (n t)").bitcast(I32))
-            word_tables[g] = table
-
-        def load_hidden(g, slot):
-            raw = keep.tile([P, PACK, J], F32, name=f"h_raw{g}", tag=slot, align_bytes=256)
-            nc.sync.dma_start(
-                out=raw[:], in_=hT[g * P * PACK : (g + 1) * P * PACK, :].rearrange("(p t) m -> p t m", t=PACK)
-            )
-            h_raw[g] = raw
-
+        word_tables = [keep.tile([P, T], I32, name=f"word_table{g}", align_bytes=256) for g in range(PASSES)]
+        h_raw = [keep.tile([P, PACK, J], F32, name=f"h_raw{g}", align_bytes=256) for g in range(PASSES)]
         scale_table = keep.tile([P, T], U8, name="scale_table", align_bytes=256)
+
+        def load_words(g):
+            nc.sync.dma_start(out=word_tables[g][:], in_=x_words[g].rearrange("p n t -> p (n t)").bitcast(I32))
+
+        def load_hidden(g):
+            rows = hT[g * P * PACK : (g + 1) * P * PACK, :]
+            nc.sync.dma_start(out=h_raw[g][:], in_=rows.rearrange("(p t) m -> p t m", t=PACK))
+
         nc.vector.memset(scale_table[:].bitcast(I32), 0)
-        load_words(0, "slot0")
+        load_words(0)
         nc.sync.dma_start(offsets[:], offs)
-        load_hidden(0, "slot2")
+        load_hidden(0)
         for q in range(4):
             (nc.scalar if q < 2 else nc.sync).dma_start(
                 out=scale_table[32 * q : 32 * q + 4 * PASSES, :].bitcast(I32),
                 in_=x_scales[:, 4 * q : 4 * q + 4, :].bitcast(I32),
             )
+        load_hidden(1)
+        load_words(1)
+        load_hidden(2)
+        load_words(2)
 
-        load_hidden(1, "slot3")
-        load_words(1, "slot1")
-        load_hidden(2, "slot5")
-        load_words(2, "slot4")
-
-        window0 = keep.tile([P, T], F32, name="window0", align_bytes=256)
-        nc.vector.memset(window0[:], UNPICKED)
-        window1 = keep.tile([P, T], F32, name="window1", align_bytes=256)
-        nc.vector.memset(window1[:], 0.0)
+        windows = [keep.tile([P, T], F32, name=f"window{m}", align_bytes=256) for m in range(2)]
+        for window in windows:
+            nc.vector.memset(window[:], 0.0)
         minus_one = keep.tile([P, 1], F32, name="minus_one")
         nc.gpsimd.memset(minus_one[:], -1.0)
 
@@ -81,7 +65,7 @@ def tile_picked_zvoc_soft_p_kernel(tc, x_words, x_scales, hT, offs, out):
         x_planes = keep.tile([P, S], U8, name="x_planes", align_bytes=64)
         h_codes = [keep.tile([P, J], U32, name=f"h_codes{g}", align_bytes=64) for g in range(PASSES)]
         h_planes = [keep.tile([P, J], U8, name=f"h_planes{g}", align_bytes=64) for g in range(PASSES)]
-        logits0 = [psum.tile([P, c.stop - c.start], F32, name=f"logits0_{i}") for i, c in enumerate(CHUNKS)]
+        logits0 = [psum.tile([P, S // 2], F32, name=f"logits0_{i}") for i in range(2)]
         logits1 = psum.tile([P, S], F32, name="logits1")
 
         def listed(entries):
@@ -91,9 +75,11 @@ def tile_picked_zvoc_soft_p_kernel(tc, x_words, x_scales, hT, offs, out):
             nc.vector.tensor_copy(x_codes[g][:, entries], word_tables[g][:].bitcast(U32).indirect(listed(entries)))
 
         def regroup(g, cols, copy):
-            width = cols.stop - cols.start
-            grouped = keep.tile([P, width, PACK], BF16, name=f"grouped{g}_{cols.start}", align_bytes=64)
-            interleave(copy, grouped[:], h_raw[g][:, :, cols])
+            grouped = keep.tile([P, cols.stop - cols.start, PACK], BF16, name=f"grouped{g}_{cols.start}", align_bytes=64)
+            copy(
+                out=grouped[:].rearrange("p (c i) t -> p c t i", i=4),
+                in_=h_raw[g][:, :, cols].rearrange("p t (c i) -> p c t i", i=4),
+            )
             return grouped
 
         def quantise(g, cols, grouped):
@@ -126,52 +112,42 @@ def tile_picked_zvoc_soft_p_kernel(tc, x_words, x_scales, hT, offs, out):
         quantise(1, tile1, regroup(1, tile1, nc.scalar.copy))
         quantise(2, tile0, last0)
         quantise(2, tile1, regroup(2, tile1, nc.scalar.copy))
-        gather_words(2, CHUNKS[0])
-        gather_words(2, slice(CHUNKS[0].stop, S))
-        for g in range(PASSES - 1):
-            for bank, entries in zip(logits0, CHUNKS):
+        for entries in HALVES:
+            gather_words(2, entries)
+        for g in range(PASSES):
+            for bank, entries in zip(logits0, HALVES):
                 multiply(g, 0, bank, entries)
             multiply(g, 1, logits1, whole)
-        multiply(2, 0, logits0[0], CHUNKS[0])
-        multiply(2, 1, logits1, whole)
-        multiply(2, 0, logits0[1], CHUNKS[1])
-        multiply(2, 0, logits0[2], CHUNKS[2])
 
-        y0 = keep.tile([P, S], F32, name="y0")
-        neg_max0 = keep.tile([P, 1], F32, name="neg_max0")
-        neg_max1 = keep.tile([P, 1], F32, name="neg_max1")
-        e1 = keep.tile([P, S], F32, name="e1", tag="exps")
-        sum0 = keep.tile([P, 1], F32, name="sum0")
-        sum1 = keep.tile([P, 1], F32, name="sum1")
-        inv0 = keep.tile([P, 1], F32, name="inv0")
-        inv1 = keep.tile([P, 1], F32, name="inv1")
-        p1 = keep.tile([P, S], F32, name="p1")
-        rows0 = keep.tile([P, T], F32, name="rows0", align_bytes=256)
+        neg_y0 = keep.tile([P, S], F32, name="neg_y0")
+        neg_max = [keep.tile([P, 1], F32, name=f"neg_max{m}") for m in range(2)]
+        exps = [keep.tile([P, S], F32, name=f"exps{m}") for m in range(2)]
+        sums = [keep.tile([P, 1], F32, name=f"sum{m}") for m in range(2)]
+        inv = [keep.tile([P, 1], F32, name=f"inv{m}") for m in range(2)]
+        rows = [keep.tile([P, T], F32, name=f"rows{m}", align_bytes=256) for m in range(2)]
 
-        for bank, entries in zip(logits0, CHUNKS):
-            nc.scalar.copy(out=y0[:, entries], in_=bank[:])
-        nc.vector.tensor_copy(window0[:].indirect(listed(CHUNKS[0])), y0[:, CHUNKS[0]])
-        nc.vector.tensor_reduce(out=neg_max1[:], in_=logits1[:], axis=AX.X, op=ALU.max, negate=True)
-        nc.vector.tensor_copy(window0[:].indirect(listed(CHUNKS[1])), y0[:, CHUNKS[1]])
-        nc.vector.tensor_reduce(out=neg_max0[:], in_=y0[:], axis=AX.X, op=ALU.max, negate=True)
-        nc.vector.tensor_copy(window0[:].indirect(listed(CHUNKS[2])), y0[:, CHUNKS[2]])
+        nc.vector.tensor_scalar(
+            out=neg_y0[:, HALVES[0]], in0=logits0[0][:], scalar1=-1.0, scalar2=None,
+            op0=ALU.mult, op1=ALU.min, accum_out=neg_max[1][:],
+        )
+        nc.vector.tensor_scalar(
+            out=neg_y0[:, HALVES[1]], in0=logits0[1][:], scalar1=-1.0, scalar2=neg_max[1][:],
+            op0=ALU.mult, op1=ALU.min, accum_out=neg_max[0][:],
+        )
+        nc.vector.tensor_reduce(out=neg_max[1][:], in_=logits1[:], axis=AX.X, op=ALU.max, negate=True)
 
-        nc.scalar.activation(out=e1[:], in_=logits1[:], func=ACT.Exp, bias=neg_max1[:], accum_out=sum1[:])
-        nc.gpsimd.tensor_tensor(out=inv1[:], in0=sum1[:], in1=minus_one[:], op=ALU.pow)
-        listed0 = keep.tile([P, S], F32, name="listed0")
-        nc.scalar.activation(out=listed0[:], in_=y0[:], func=ACT.Exp, bias=neg_max0[:], accum_out=sum0[:])
-        nc.gpsimd.tensor_tensor(out=inv0[:], in0=sum0[:], in1=minus_one[:], op=ALU.pow)
-        nc.scalar.activation(out=p1[:], in_=e1[:], func=ACT.Copy, scale=inv1[:])
-        nc.vector.tensor_copy(window1[:].indirect(offsets[:]), p1[:])
+        nc.scalar.activation(out=exps[0][:], in_=neg_y0[:], func=ACT.Exp, scale=-1.0, bias=neg_max[0][:], accum_out=sums[0][:])
+        nc.scalar.activation(out=exps[1][:], in_=logits1[:], func=ACT.Exp, bias=neg_max[1][:], accum_out=sums[1][:])
+        for m in range(2):
+            nc.gpsimd.tensor_tensor(out=inv[m][:], in0=sums[m][:], in1=minus_one[:], op=ALU.pow)
 
-        e0 = keep.tile([P, T], F32, name="e0", tag="exps")
-        for i in range(len(PIECES) + 1):
-            if i < len(PIECES):
-                cols = PIECES[i]
-                nc.scalar.activation(out=e0[:, cols], in_=window0[:, cols], func=ACT.Exp, bias=neg_max0[:])
-            if i > 0:
-                cols = PIECES[i - 1]
-                nc.scalar.activation(out=rows0[:, cols], in_=e0[:, cols], func=ACT.Copy, scale=inv0[:])
-                nc.scalar.dma_start(out=out[0:P, cols], in_=rows0[:, cols])
-        nc.sync.dma_start(out=out[P:J:2, :], in_=window1[0:P:2, :])
-        nc.scalar.dma_start(out=out[P + 1 : J : 2, :], in_=window1[1:P:2, :])
+        nc.vector.tensor_copy(windows[0][:].indirect(offsets[:]), exps[0][:])
+        for entries in HALVES:
+            nc.scalar.activation(out=windows[1][:].indirect(listed(entries)), in_=exps[1][:, entries], func=ACT.Copy)
+
+        for m in range(2):
+            for cols in COLUMN_HALVES:
+                nc.vector.tensor_scalar(
+                    out=rows[m][:, cols], in0=windows[m][:, cols], scalar1=inv[m][:], scalar2=None, op0=ALU.mult
+                )
+                nc.sync.dma_start(out=out[m * P : (m + 1) * P, cols], in_=rows[m][:, cols])

@@ -20,7 +20,8 @@ P = 128
 PACK = 4
 PASSES = K // (P * PACK)
 HALVES = (slice(0, S // 2), slice(S // 2, S))
-COLUMN_HALVES = (slice(0, T // 2), slice(T // 2, T))
+MARGIN = 40.0
+COLUMN_HALVES = (slice(0, 320), slice(320, T))
 
 
 def tile_picked_zvoc_soft_p_kernel(tc, x_words, x_scales, hT, offs, out):
@@ -65,14 +66,19 @@ def tile_picked_zvoc_soft_p_kernel(tc, x_words, x_scales, hT, offs, out):
         x_planes = keep.tile([P, S], U8, name="x_planes", align_bytes=64)
         h_codes = [keep.tile([P, J], U32, name=f"h_codes{g}", align_bytes=64) for g in range(PASSES)]
         h_planes = [keep.tile([P, J], U8, name=f"h_planes{g}", align_bytes=64) for g in range(PASSES)]
-        logits0 = [psum.tile([P, S // 2], F32, name=f"logits0_{i}") for i in range(2)]
-        logits1 = psum.tile([P, S], F32, name="logits1")
+        logits = [[psum.tile([P, S // 2], F32, name=f"logits{m}_{i}") for i in range(2)] for m in range(2)]
 
         def listed(entries):
             return offsets[:, entries.start // 16 : entries.stop // 16]
 
         def gather_words(g, entries):
             nc.vector.tensor_copy(x_codes[g][:, entries], word_tables[g][:].bitcast(U32).indirect(listed(entries)))
+
+        def negate_on_scalar(out, in_):
+            nc.scalar.activation(out=out, in_=in_, func=ACT.Copy, scale=-1.0)
+
+        def negate_on_vector(out, in_):
+            nc.vector.tensor_scalar(out=out, in0=in_, scalar1=-1.0, scalar2=None, op0=ALU.mult)
 
         def regroup(g, cols, copy):
             grouped = keep.tile([P, cols.stop - cols.start, PACK], BF16, name=f"grouped{g}_{cols.start}", align_bytes=64)
@@ -105,45 +111,69 @@ def tile_picked_zvoc_soft_p_kernel(tc, x_words, x_scales, hT, offs, out):
         gather_words(0, whole)
         nc.vector.tensor_copy(x_planes[:], scale_table[:].indirect(offsets[:]))
         both, tile0, tile1 = slice(0, J), slice(0, P), slice(P, J)
-        quantise(0, both, regroup(0, both, nc.scalar.copy))
-        quantise(1, tile0, regroup(1, tile0, nc.scalar.copy))
+        quantise(0, both, regroup(0, both, negate_on_scalar))
+        quantise(1, tile0, regroup(1, tile0, negate_on_scalar))
         gather_words(1, whole)
-        last0 = regroup(2, tile0, nc.vector.tensor_copy)
-        quantise(1, tile1, regroup(1, tile1, nc.scalar.copy))
+        last0 = regroup(2, tile0, negate_on_vector)
+        quantise(1, tile1, regroup(1, tile1, negate_on_scalar))
         quantise(2, tile0, last0)
-        quantise(2, tile1, regroup(2, tile1, nc.scalar.copy))
+        quantise(2, tile1, regroup(2, tile1, negate_on_scalar))
         for entries in HALVES:
             gather_words(2, entries)
         for g in range(PASSES):
-            for bank, entries in zip(logits0, HALVES):
-                multiply(g, 0, bank, entries)
-            multiply(g, 1, logits1, whole)
+            for i, entries in enumerate(HALVES):
+                for m in range(2):
+                    multiply(g, m, logits[m][i], entries)
 
-        neg_y0 = keep.tile([P, S], F32, name="neg_y0")
-        neg_max = [keep.tile([P, 1], F32, name=f"neg_max{m}") for m in range(2)]
+        shifted = [keep.tile([P, S // 2], F32, name=f"shifted{m}") for m in range(2)]
+        bias = {(m, i): keep.tile([P, 1], F32, name=f"bias{m}_{i}")[:] for m, i in ((0, 1), (1, 0), (1, 1))}
+        bias[0, 0] = shifted[1][:, 0:1]
         exps = [keep.tile([P, S], F32, name=f"exps{m}") for m in range(2)]
+        half_sums = [[keep.tile([P, 1], F32, name=f"half_sum{m}_{i}") for i in range(2)] for m in range(2)]
         sums = [keep.tile([P, 1], F32, name=f"sum{m}") for m in range(2)]
         inv = [keep.tile([P, 1], F32, name=f"inv{m}") for m in range(2)]
         rows = [keep.tile([P, T], F32, name=f"rows{m}", align_bytes=256) for m in range(2)]
 
-        nc.vector.tensor_scalar(
-            out=neg_y0[:, HALVES[0]], in0=logits0[0][:], scalar1=-1.0, scalar2=None,
-            op0=ALU.mult, op1=ALU.min, accum_out=neg_max[1][:],
-        )
-        nc.vector.tensor_scalar(
-            out=neg_y0[:, HALVES[1]], in0=logits0[1][:], scalar1=-1.0, scalar2=neg_max[1][:],
-            op0=ALU.mult, op1=ALU.min, accum_out=neg_max[0][:],
-        )
-        nc.vector.tensor_reduce(out=neg_max[1][:], in_=logits1[:], axis=AX.X, op=ALU.max, negate=True)
+        def first_bias(m):
+            nc.vector.tensor_reduce(out=bias[m, 0], in_=logits[m][0][:], axis=AX.X, op=ALU.min)
 
-        nc.scalar.activation(out=exps[0][:], in_=neg_y0[:], func=ACT.Exp, scale=-1.0, bias=neg_max[0][:], accum_out=sums[0][:])
-        nc.scalar.activation(out=exps[1][:], in_=logits1[:], func=ACT.Exp, bias=neg_max[1][:], accum_out=sums[1][:])
-        for m in range(2):
+        def second_bias(m):
+            nc.vector.tensor_scalar(
+                out=shifted[m][:], in0=logits[m][1][:], scalar1=MARGIN, scalar2=bias[m, 0],
+                op0=ALU.add, op1=ALU.min, accum_out=bias[m, 1],
+            )
+
+        def exponentiate(m, i):
+            nc.scalar.activation(
+                out=exps[m][:, HALVES[i]], in_=logits[m][i][:], func=ACT.Exp, scale=-1.0, bias=bias[m, i],
+                accum_out=half_sums[m][i][:],
+            )
+
+        def scatter(m, i):
+            target = windows[m][:].indirect(listed(HALVES[i]))
+            if m == 0:
+                nc.vector.tensor_copy(target, exps[0][:, HALVES[i]])
+            else:
+                nc.scalar.activation(out=target, in_=exps[1][:, HALVES[i]], func=ACT.Copy)
+
+        def invert_sum(m):
+            nc.gpsimd.tensor_tensor(out=sums[m][:], in0=half_sums[m][0][:], in1=half_sums[m][1][:], op=ALU.add)
             nc.gpsimd.tensor_tensor(out=inv[m][:], in0=sums[m][:], in1=minus_one[:], op=ALU.pow)
 
-        nc.vector.tensor_copy(windows[0][:].indirect(offsets[:]), exps[0][:])
-        for entries in HALVES:
-            nc.scalar.activation(out=windows[1][:].indirect(listed(entries)), in_=exps[1][:, entries], func=ACT.Copy)
+        first_bias(0)
+        first_bias(1)
+        second_bias(0)
+        exponentiate(0, 0)
+        exponentiate(1, 0)
+        exponentiate(0, 1)
+        scatter(0, 0)
+        second_bias(1)
+        scatter(1, 0)
+        exponentiate(1, 1)
+        invert_sum(0)
+        scatter(0, 1)
+        scatter(1, 1)
+        invert_sum(1)
 
         for m in range(2):
             for cols in COLUMN_HALVES:

@@ -20,8 +20,11 @@ P = 128
 PACK = 4
 PASSES = K // (P * PACK)
 HALVES = (slice(0, S // 2), slice(S // 2, S))
+VECTOR_RUNS = (slice(0, 128), slice(128, S))
+HALF = S // 2
+EXP_RUNS = ((slice(0, 128), slice(128, HALF), HALVES[1]), HALVES)
 MARGIN = 40.0
-COLUMN_HALVES = (slice(0, 320), slice(320, T))
+COLUMN_PIECES = ((slice(0, 320), slice(320, T)), (slice(0, 320), slice(320, T)))
 
 
 def tile_picked_zvoc_soft_p_kernel(tc, x_words, x_scales, hT, offs, out):
@@ -126,11 +129,10 @@ def tile_picked_zvoc_soft_p_kernel(tc, x_words, x_scales, hT, offs, out):
                     multiply(g, m, logits[m][i], entries)
 
         shifted = [keep.tile([P, S // 2], F32, name=f"shifted{m}") for m in range(2)]
-        bias = {(m, i): keep.tile([P, 1], F32, name=f"bias{m}_{i}")[:] for m, i in ((0, 1), (1, 0), (1, 1))}
-        bias[0, 0] = shifted[1][:, 0:1]
+        bias = {(m, i): keep.tile([P, 1], F32, name=f"bias{m}_{i}")[:] for m, i in ((0, 0), (1, 0), (1, 1))}
+        bias[0, 1] = shifted[1][:, 0:1]
         exps = [keep.tile([P, S], F32, name=f"exps{m}") for m in range(2)]
-        half_sums = [[keep.tile([P, 1], F32, name=f"half_sum{m}_{i}") for i in range(2)] for m in range(2)]
-        sums = [keep.tile([P, 1], F32, name=f"sum{m}") for m in range(2)]
+        part_sums = [[keep.tile([P, 1], F32, name=f"part_sum{m}_{j}") for j in range(len(EXP_RUNS[m]))] for m in range(2)]
         inv = [keep.tile([P, 1], F32, name=f"inv{m}") for m in range(2)]
         rows = [keep.tile([P, T], F32, name=f"rows{m}", align_bytes=256) for m in range(2)]
 
@@ -143,29 +145,35 @@ def tile_picked_zvoc_soft_p_kernel(tc, x_words, x_scales, hT, offs, out):
                 op0=ALU.add, op1=ALU.min, accum_out=bias[m, 1],
             )
 
-        def exponentiate(m, i):
+        def exponentiate(m, j):
+            entries = EXP_RUNS[m][j]
+            i = entries.start // HALF
             nc.scalar.activation(
-                out=exps[m][:, HALVES[i]], in_=logits[m][i][:], func=ACT.Exp, scale=-1.0, bias=bias[m, i],
-                accum_out=half_sums[m][i][:],
+                out=exps[m][:, entries], in_=logits[m][i][:, entries.start - i * HALF : entries.stop - i * HALF],
+                func=ACT.Exp, scale=-1.0, bias=bias[m, i], accum_out=part_sums[m][j][:],
             )
 
         def scatter(m, i):
-            target = windows[m][:].indirect(listed(HALVES[i]))
             if m == 0:
-                nc.vector.tensor_copy(target, exps[0][:, HALVES[i]])
+                nc.vector.tensor_copy(windows[0][:].indirect(listed(VECTOR_RUNS[i])), exps[0][:, VECTOR_RUNS[i]])
             else:
-                nc.scalar.activation(out=target, in_=exps[1][:, HALVES[i]], func=ACT.Copy)
+                nc.scalar.activation(out=windows[1][:].indirect(listed(HALVES[i])), in_=exps[1][:, HALVES[i]], func=ACT.Copy)
 
         def invert_sum(m):
-            nc.gpsimd.tensor_tensor(out=sums[m][:], in0=half_sums[m][0][:], in1=half_sums[m][1][:], op=ALU.add)
-            nc.gpsimd.tensor_tensor(out=inv[m][:], in0=sums[m][:], in1=minus_one[:], op=ALU.pow)
+            total = part_sums[m][0]
+            for j in range(1, len(EXP_RUNS[m])):
+                more = keep.tile([P, 1], F32, name=f"sum{m}_{j}")
+                nc.gpsimd.tensor_tensor(out=more[:], in0=total[:], in1=part_sums[m][j][:], op=ALU.add)
+                total = more
+            nc.gpsimd.tensor_tensor(out=inv[m][:], in0=total[:], in1=minus_one[:], op=ALU.pow)
 
         first_bias(0)
         first_bias(1)
         second_bias(0)
         exponentiate(0, 0)
-        exponentiate(1, 0)
         exponentiate(0, 1)
+        exponentiate(1, 0)
+        exponentiate(0, 2)
         scatter(0, 0)
         second_bias(1)
         scatter(1, 0)
@@ -176,7 +184,7 @@ def tile_picked_zvoc_soft_p_kernel(tc, x_words, x_scales, hT, offs, out):
         invert_sum(1)
 
         for m in range(2):
-            for cols in COLUMN_HALVES:
+            for cols in COLUMN_PIECES[m]:
                 nc.vector.tensor_scalar(
                     out=rows[m][:, cols], in0=windows[m][:, cols], scalar1=inv[m][:], scalar2=None, op0=ALU.mult
                 )

@@ -129,8 +129,8 @@ def tile_picked_zvoc_soft_p_kernel(tc, x_words, x_scales, hT, offs, out):
                     multiply(g, m, logits[m][i], entries)
 
         shifted = [keep.tile([P, S // 2], F32, name=f"shifted{m}") for m in range(2)]
-        bias = {(m, i): keep.tile([P, 1], F32, name=f"bias{m}_{i}")[:] for m, i in ((0, 0), (1, 0), (1, 1))}
-        bias[0, 1] = shifted[1][:, 0:1]
+        bias = {(m, i): keep.tile([P, 1], F32, name=f"bias{m}_{i}")[:] for m, i in ((0, 0), (1, 0), (0, 1))}
+        bias[1, 1] = bias[0, 1]
         exps = [keep.tile([P, S], F32, name=f"exps{m}") for m in range(2)]
         part_sums = [[keep.tile([P, 1], F32, name=f"part_sum{m}_{j}") for j in range(len(EXP_RUNS[m]))] for m in range(2)]
         inv = [keep.tile([P, 1], F32, name=f"inv{m}") for m in range(2)]

@@ -1,3 +1,4 @@
+import math
 from contextlib import ExitStack
 
 import concourse.mybir as mybir
@@ -20,10 +21,11 @@ P = 128
 PACK = 4
 PASSES = K // (P * PACK)
 HALVES = (slice(0, S // 2), slice(S // 2, S))
-VECTOR_RUNS = (slice(0, 128), slice(128, S))
+VECTOR_RUNS = (slice(0, 192), slice(192, S))
 HALF = S // 2
-EXP_RUNS = ((slice(0, 128), slice(128, HALF), HALVES[1]), HALVES)
-MARGIN = 40.0
+EXP_RUNS = ((slice(0, 192), slice(192, HALF), HALVES[1]), HALVES)
+GROW = 2.0**58
+MARGIN = math.log(GROW)
 COLUMN_PIECES = ((slice(0, 320), slice(320, T)), (slice(0, 320), slice(320, T)))
 
 
@@ -128,7 +130,8 @@ def tile_picked_zvoc_soft_p_kernel(tc, x_words, x_scales, hT, offs, out):
                 for m in range(2):
                     multiply(g, m, logits[m][i], entries)
 
-        shifted = [keep.tile([P, S // 2], F32, name=f"shifted{m}") for m in range(2)]
+        below = [keep.tile([P, HALF], F32, name=f"below{m}") for m in range(2)]
+        small = keep.tile([P, HALF], F32, name="small")
         bias = {(m, i): keep.tile([P, 1], F32, name=f"bias{m}_{i}")[:] for m, i in ((0, 0), (1, 0), (0, 1))}
         bias[1, 1] = bias[0, 1]
         exps = [keep.tile([P, S], F32, name=f"exps{m}") for m in range(2)]
@@ -141,30 +144,37 @@ def tile_picked_zvoc_soft_p_kernel(tc, x_words, x_scales, hT, offs, out):
 
         def second_bias(m):
             nc.vector.tensor_scalar(
-                out=shifted[m][:], in0=logits[m][1][:], scalar1=MARGIN, scalar2=bias[m, 0],
-                op0=ALU.add, op1=ALU.min, accum_out=bias[m, 1],
+                out=below[m][:], in0=logits[m][1][:], scalar1=bias[m, 0], scalar2=-MARGIN,
+                op0=ALU.subtract, op1=ALU.min, accum_out=bias[m, 1],
             )
 
         def exponentiate(m, j):
             entries = EXP_RUNS[m][j]
             i = entries.start // HALF
             nc.scalar.activation(
-                out=exps[m][:, entries], in_=logits[m][i][:, entries.start - i * HALF : entries.stop - i * HALF],
+                out=small[:] if (m, i) == (0, 1) else exps[m][:, entries],
+                in_=below[m][:] if i else logits[m][0][:, entries],
                 func=ACT.Exp, scale=-1.0, bias=bias[m, i], accum_out=part_sums[m][j][:],
             )
 
         def scatter(m, i):
-            if m == 0:
-                nc.vector.tensor_copy(windows[0][:].indirect(listed(VECTOR_RUNS[i])), exps[0][:, VECTOR_RUNS[i]])
+            if m == 1:
+                nc.scalar.activation(
+                    out=windows[1][:].indirect(listed(HALVES[i])), in_=exps[1][:, HALVES[i]], func=ACT.Copy,
+                    scale=GROW if i else 1.0,
+                )
             else:
-                nc.scalar.activation(out=windows[1][:].indirect(listed(HALVES[i])), in_=exps[1][:, HALVES[i]], func=ACT.Copy)
+                nc.vector.tensor_copy(windows[0][:].indirect(listed(VECTOR_RUNS[i])), exps[0][:, VECTOR_RUNS[i]])
 
         def invert_sum(m):
-            total = part_sums[m][0]
-            for j in range(1, len(EXP_RUNS[m])):
-                more = keep.tile([P, 1], F32, name=f"sum{m}_{j}")
-                nc.gpsimd.tensor_tensor(out=more[:], in0=total[:], in1=part_sums[m][j][:], op=ALU.add)
-                total = more
+            first = part_sums[m][0]
+            if m == 0:
+                first = keep.tile([P, 1], F32, name="first_half_sum0")
+                nc.gpsimd.tensor_tensor(out=first[:], in0=part_sums[0][0][:], in1=part_sums[0][1][:], op=ALU.add)
+            total = keep.tile([P, 1], F32, name=f"sum{m}")
+            nc.gpsimd.tensor_scalar(
+                out=total[:], in0=part_sums[m][-1][:], scalar1=GROW, scalar2=first[:], op0=ALU.mult, op1=ALU.add
+            )
             nc.gpsimd.tensor_tensor(out=inv[m][:], in0=total[:], in1=minus_one[:], op=ALU.pow)
 
         first_bias(0)
@@ -174,6 +184,7 @@ def tile_picked_zvoc_soft_p_kernel(tc, x_words, x_scales, hT, offs, out):
         exponentiate(0, 1)
         exponentiate(1, 0)
         exponentiate(0, 2)
+        nc.gpsimd.tensor_scalar(out=exps[0][:, HALVES[1]], in0=small[:], scalar1=GROW, scalar2=0.0, op0=ALU.mult, op1=ALU.add)
         scatter(0, 0)
         second_bias(1)
         scatter(1, 0)

@@ -64,8 +64,6 @@ def tile_picked_zvoc_soft_p_kernel(tc, x_words, x_scales, hT, offs, out):
         windows = [keep.tile([P, T], F32, name=f"window{m}", align_bytes=256) for m in range(2)]
         for window in windows:
             nc.vector.memset(window[:], 0.0)
-        minus_one = keep.tile([P, 1], F32, name="minus_one")
-        nc.gpsimd.memset(minus_one[:], -1.0)
 
         x_codes = [keep.tile([P, S], U32, name=f"x_codes{g}", align_bytes=64) for g in range(PASSES)]
         x_planes = keep.tile([P, S], U8, name="x_planes", align_bytes=64)
@@ -136,7 +134,8 @@ def tile_picked_zvoc_soft_p_kernel(tc, x_words, x_scales, hT, offs, out):
         bias[1, 1] = bias[0, 1]
         exps = [keep.tile([P, S], F32, name=f"exps{m}") for m in range(2)]
         part_sums = [[keep.tile([P, 1], F32, name=f"part_sum{m}_{j}") for j in range(len(EXP_RUNS[m]))] for m in range(2)]
-        inv = [keep.tile([P, 1], F32, name=f"inv{m}") for m in range(2)]
+        totals = keep.tile([P, 2], F32, name="totals")
+        inv = keep.tile([P, 2], F32, name="inv")
         rows = [keep.tile([P, T], F32, name=f"rows{m}", align_bytes=256) for m in range(2)]
 
         def first_bias(m):
@@ -166,17 +165,6 @@ def tile_picked_zvoc_soft_p_kernel(tc, x_words, x_scales, hT, offs, out):
             else:
                 nc.vector.tensor_copy(windows[0][:].indirect(listed(VECTOR_RUNS[i])), exps[0][:, VECTOR_RUNS[i]])
 
-        def invert_sum(m):
-            first = part_sums[m][0]
-            if m == 0:
-                first = keep.tile([P, 1], F32, name="first_half_sum0")
-                nc.gpsimd.tensor_tensor(out=first[:], in0=part_sums[0][0][:], in1=part_sums[0][1][:], op=ALU.add)
-            total = keep.tile([P, 1], F32, name=f"sum{m}")
-            nc.gpsimd.tensor_scalar(
-                out=total[:], in0=part_sums[m][-1][:], scalar1=GROW, scalar2=first[:], op0=ALU.mult, op1=ALU.add
-            )
-            nc.gpsimd.tensor_tensor(out=inv[m][:], in0=total[:], in1=minus_one[:], op=ALU.pow)
-
         first_bias(0)
         first_bias(1)
         second_bias(0)
@@ -189,14 +177,19 @@ def tile_picked_zvoc_soft_p_kernel(tc, x_words, x_scales, hT, offs, out):
         second_bias(1)
         scatter(1, 0)
         exponentiate(1, 1)
-        invert_sum(0)
+        first_half_sum0 = keep.tile([P, 1], F32, name="first_half_sum0")
+        nc.gpsimd.tensor_tensor(out=first_half_sum0[:], in0=part_sums[0][0][:], in1=part_sums[0][1][:], op=ALU.add)
+        nc.gpsimd.tensor_scalar(
+            out=totals[:, 0:1], in0=part_sums[0][2][:], scalar1=GROW, scalar2=first_half_sum0[:], op0=ALU.mult, op1=ALU.add
+        )
+        nc.scalar.activation(out=totals[:, 1:2], in_=part_sums[1][1][:], func=ACT.Identity, scale=GROW, bias=part_sums[1][0][:])
         scatter(0, 1)
         scatter(1, 1)
-        invert_sum(1)
+        nc.vector.reciprocal(out=inv[:], in_=totals[:])
 
         for m in range(2):
             for cols in COLUMN_PIECES[m]:
                 nc.vector.tensor_scalar(
-                    out=rows[m][:, cols], in0=windows[m][:, cols], scalar1=inv[m][:], scalar2=None, op0=ALU.mult
+                    out=rows[m][:, cols], in0=windows[m][:, cols], scalar1=inv[:, m : m + 1], scalar2=None, op0=ALU.mult
                 )
                 nc.sync.dma_start(out=out[m * P : (m + 1) * P, cols], in_=rows[m][:, cols])

import math
from contextlib import ExitStack

import concourse.mybir as mybir

K, T, S, J = 1536, 1024, 512, 256
FLOPS = 2 * K * S * J

F32 = mybir.dt.float32
BF16 = mybir.dt.bfloat16
I32 = mybir.dt.int32
U32 = mybir.dt.uint32
U16 = mybir.dt.uint16
U8 = mybir.dt.uint8
FP8X4 = mybir.dt.float8_e4m3fn_x4
ACT = mybir.ActivationFunctionType
ALU = mybir.AluOpType
AX = mybir.AxisListType

P = 128
PACK = 4
PASSES = K // (P * PACK)
HALVES = (slice(0, S // 2), slice(S // 2, S))
VECTOR_RUNS = (slice(0, 192), slice(192, S))
HALF = S // 2
EXP_RUNS = ((slice(0, 192), slice(192, HALF), HALVES[1]), HALVES)
GROW = 2.0**58
MARGIN = math.log(GROW)
COLUMN_PIECES = ((slice(0, 320), slice(320, T)), (slice(0, 320), slice(320, T)))


def tile_picked_zvoc_soft_p_kernel(tc, x_words, x_scales, hT, offs, out):
    nc = tc.nc
    with ExitStack() as ctx:
        keep = ctx.enter_context(tc.tile_pool(name="keep", bufs=1))
        psum = ctx.enter_context(tc.psum_pool(name="psum", bufs=1))

        offsets = keep.tile([P, S // 16], U16, name="offsets")
        word_tables = [keep.tile([P, T], I32, name=f"word_table{g}", align_bytes=256) for g in range(PASSES)]
        h_raw = [keep.tile([P, PACK, J], F32, name=f"h_raw{g}", align_bytes=256) for g in range(PASSES)]
        scale_table = keep.tile([P, T], U8, name="scale_table", align_bytes=256)

        def load_words(g):
            nc.sync.dma_start(out=word_tables[g][:], in_=x_words[g].rearrange("p n t -> p (n t)").bitcast(I32))

        def load_hidden(g):
            rows = hT[g * P * PACK : (g + 1) * P * PACK, :]
            nc.sync.dma_start(out=h_raw[g][:], in_=rows.rearrange("(p t) m -> p t m", t=PACK))

        nc.vector.memset(scale_table[:].bitcast(I32), 0)
        load_words(0)
        nc.sync.dma_start(offsets[:], offs)
        load_hidden(0)
        for q in range(4):
            (nc.scalar if q < 2 else nc.sync).dma_start(
                out=scale_table[32 * q : 32 * q + 4 * PASSES, :].bitcast(I32),
                in_=x_scales[:, 4 * q : 4 * q + 4, :].bitcast(I32),
            )
        load_hidden(1)
        load_words(1)
        load_hidden(2)
        load_words(2)

        windows = [keep.tile([P, T], F32, name=f"window{m}", align_bytes=256) for m in range(2)]
        for window in windows:
            nc.vector.memset(window[:], 0.0)

        x_codes = [keep.tile([P, S], U32, name=f"x_codes{g}", align_bytes=64) for g in range(PASSES)]
        x_planes = keep.tile([P, S], U8, name="x_planes", align_bytes=64)
        h_codes = [keep.tile([P, J], U32, name=f"h_codes{g}", align_bytes=64) for g in range(PASSES)]
        h_planes = [keep.tile([P, J], U8, name=f"h_planes{g}", align_bytes=64) for g in range(PASSES)]
        logits = [[psum.tile([P, S // 2], F32, name=f"logits{m}_{i}") for i in range(2)] for m in range(2)]

        def listed(entries):
            return offsets[:, entries.start // 16 : entries.stop // 16]

        def gather_words(g, entries):
            nc.vector.tensor_copy(x_codes[g][:, entries], word_tables[g][:].bitcast(U32).indirect(listed(entries)))

        def negate_on_scalar(out, in_):
            nc.scalar.activation(out=out, in_=in_, func=ACT.Copy, scale=-1.0)

        def negate_on_vector(out, in_):
            nc.vector.tensor_scalar(out=out, in0=in_, scalar1=-1.0, scalar2=None, op0=ALU.mult)

        def regroup(g, cols, copy):
            grouped = keep.tile([P, cols.stop - cols.start, PACK], BF16, name=f"grouped{g}_{cols.start}", align_bytes=64)
            copy(
                out=grouped[:].rearrange("p (c i) t -> p c t i", i=4),
                in_=h_raw[g][:, :, cols].rearrange("p t (c i) -> p c t i", i=4),
            )
            return grouped

        def quantise(g, cols, grouped):
            nc.vector.quantize_mx(
                out=h_codes[g][:, cols].bitcast(FP8X4),
                scales=h_planes[g][:, cols],
                in_=grouped[:].rearrange("p c t -> p (c t)"),
            )

        def multiply(g, m, bank, entries):
            cols = slice(m * P, (m + 1) * P)
            nc.tensor.matmul_mx(
                out=bank[:],
                lhsT=h_codes[g][:, cols].bitcast(FP8X4),
                lhsT_scale=h_planes[g][:, cols],
                rhs=x_codes[g][:, entries].bitcast(FP8X4),
                rhs_scale=x_planes[4 * g :, entries],
                start=(g == 0),
                stop=(g == PASSES - 1),
            )

        whole = slice(0, S)
        gather_words(0, whole)
        nc.vector.tensor_copy(x_planes[:], scale_table[:].indirect(offsets[:]))
        both, tile0, tile1 = slice(0, J), slice(0, P), slice(P, J)
        quantise(0, both, regroup(0, both, negate_on_scalar))
        quantise(1, tile0, regroup(1, tile0, negate_on_scalar))
        gather_words(1, whole)
        last0 = regroup(2, tile0, negate_on_vector)
        quantise(1, tile1, regroup(1, tile1, negate_on_scalar))
        quantise(2, tile0, last0)
        quantise(2, tile1, regroup(2, tile1, negate_on_scalar))
        for entries in HALVES:
            gather_words(2, entries)
        for g in range(PASSES):
            for i, entries in enumerate(HALVES):
                for m in range(2):
                    multiply(g, m, logits[m][i], entries)

        below = [keep.tile([P, HALF], F32, name=f"below{m}") for m in range(2)]
        small = keep.tile([P, HALF], F32, name="small")
        bias = {(m, i): keep.tile([P, 1], F32, name=f"bias{m}_{i}")[:] for m, i in ((0, 0), (1, 0), (0, 1))}
        bias[1, 1] = bias[0, 1]
        exps = [keep.tile([P, S], F32, name=f"exps{m}") for m in range(2)]
        part_sums = [[keep.tile([P, 1], F32, name=f"part_sum{m}_{j}") for j in range(len(EXP_RUNS[m]))] for m in range(2)]
        totals = keep.tile([P, 2], F32, name="totals")
        inv = keep.tile([P, 2], F32, name="inv")
        rows = [keep.tile([P, T], F32, name=f"rows{m}", align_bytes=256) for m in range(2)]

        def first_bias(m):
            nc.vector.tensor_reduce(out=bias[m, 0], in_=logits[m][0][:], axis=AX.X, op=ALU.min)

        def second_bias(m):
            nc.vector.tensor_scalar(
                out=below[m][:], in0=logits[m][1][:], scalar1=bias[m, 0], scalar2=-MARGIN,
                op0=ALU.subtract, op1=ALU.min, accum_out=bias[m, 1],
            )

        def exponentiate(m, j):
            entries = EXP_RUNS[m][j]
            i = entries.start // HALF
            nc.scalar.activation(
                out=small[:] if (m, i) == (0, 1) else exps[m][:, entries],
                in_=below[m][:] if i else logits[m][0][:, entries],
                func=ACT.Exp, scale=-1.0, bias=bias[m, i], accum_out=part_sums[m][j][:],
            )

        def scatter(m, i):
            if m == 1:
                nc.scalar.activation(
                    out=windows[1][:].indirect(listed(HALVES[i])), in_=exps[1][:, HALVES[i]], func=ACT.Copy,
                    scale=GROW if i else 1.0,
                )
            else:
                nc.vector.tensor_copy(windows[0][:].indirect(listed(VECTOR_RUNS[i])), exps[0][:, VECTOR_RUNS[i]])

        first_bias(0)
        first_bias(1)
        second_bias(0)
        exponentiate(0, 0)
        exponentiate(0, 1)
        exponentiate(1, 0)
        exponentiate(0, 2)
        nc.gpsimd.tensor_scalar(out=exps[0][:, HALVES[1]], in0=small[:], scalar1=GROW, scalar2=0.0, op0=ALU.mult, op1=ALU.add)
        scatter(0, 0)
        second_bias(1)
        scatter(1, 0)
        exponentiate(1, 1)
        first_half_sum0 = keep.tile([P, 1], F32, name="first_half_sum0")
        nc.gpsimd.tensor_tensor(out=first_half_sum0[:], in0=part_sums[0][0][:], in1=part_sums[0][1][:], op=ALU.add)
        nc.gpsimd.tensor_scalar(
            out=totals[:, 0:1], in0=part_sums[0][2][:], scalar1=GROW, scalar2=first_half_sum0[:], op0=ALU.mult, op1=ALU.add
        )
        nc.scalar.activation(out=totals[:, 1:2], in_=part_sums[1][1][:], func=ACT.Identity, scale=GROW, bias=part_sums[1][0][:])
        scatter(0, 1)
        scatter(1, 1)
        nc.vector.reciprocal(out=inv[:], in_=totals[:])

        for m in range(2):
            for cols in COLUMN_PIECES[m]:
                nc.vector.tensor_scalar(
                    out=rows[m][:, cols], in0=windows[m][:, cols], scalar1=inv[:, m : m + 1], scalar2=None, op0=ALU.mult
                )
                nc.sync.dma_start(out=out[m * P : (m + 1) * P, cols], in_=rows[m][:, cols])
